import numpy as np
import ml_dtypes


def mxq(x, axis, fmt="e4m3"):
    dtype, down = {"e4m3": (ml_dtypes.float8_e4m3fn, 7), "e5m2": (ml_dtypes.float8_e5m2, 14)}[fmt]
    v = np.moveaxis(np.asarray(x, np.float32).astype(ml_dtypes.bfloat16).astype(np.float64), axis, -1)
    blocks = v.reshape(v.shape[:-1] + (-1, 32))
    amax = np.abs(blocks).max(-1, keepdims=True)
    byte = np.maximum(np.where(amax > 0, np.frexp(amax)[1] - 1 + 127, 0) - down, 1)
    scale = np.exp2(byte - 127.0)
    codes = (blocks / scale).astype(np.float32).astype(dtype).astype(np.float64)
    return np.moveaxis((codes * scale).reshape(v.shape), -1, axis)


WIDE = False


def mx_kscale(k):
    if not WIDE:
        return np.ones(k)
    levels = np.array([30, -30])
    if k % 512:
        return np.exp2(np.random.permutation(np.resize(levels, k // 32))).repeat(32)
    a = np.empty((k // 512, 16))
    for p in range(k // 512):
        a[p, :8] = np.random.permutation(np.resize(levels, 8))
        for g in range(8):
            far = levels[np.abs(levels - a[p, g]) >= 10]
            a[p, g + 8] = far[np.random.randint(len(far))]
    return np.exp2(a.ravel()).repeat(32)


def f64(x):
    return np.asarray(x).astype(np.float64)


def striped(idx):
    return np.tile(np.asarray(idx).reshape(-1, 16).T, (8, 1)).astype(np.uint16)


def unstriped(offs):
    return offs[:16].T.reshape(-1).astype(np.int64)


def striped8(idx):
    return np.asarray(idx).reshape(8, -1, 16).transpose(0, 2, 1).reshape(128, -1).astype(np.uint16)


def unstriped8(offs):
    return offs.reshape(8, 16, -1).transpose(0, 2, 1).reshape(8, -1).astype(np.int64)


def pick8(x, idx, run):
    r = np.arange(len(x))
    return x[r[:, None], idx[r % (8 * run) // run]]


E2M1 = np.array([0.0, 0.5, 1.0, 1.5, 2.0, 3.0, 4.0, 6.0, -0.0, -0.5, -1.0, -1.5, -2.0, -3.0, -4.0, -6.0])


def pack_weight(w, fmt):
    k, n = w.shape
    w = f64(np.asarray(w, np.float32).astype(ml_dtypes.bfloat16)).reshape(k // 32, 32, n)
    amax = np.abs(w).max(1)
    if fmt in ("e4m3", "e5m2"):
        byte = np.frexp(amax)[1] - 1 + 127 - (7 if fmt == "e4m3" else 14)
    else:
        mant, ex = np.frexp(amax / 6.0)
        byte = np.where(mant > 0.5, ex, ex - 1) + 127
    byte = np.clip(np.where(amax > 0, byte, 1), 1, 254)
    scaled = (w * np.exp2(127.0 - byte)[:, None, :]).reshape(k, n).astype(np.float32)
    by_word = np.ascontiguousarray(scaled.reshape(k // 512, 128, 4, n).transpose(0, 1, 3, 2))
    if fmt in ("e4m3", "e5m2"):
        words = by_word.astype(ml_dtypes.float8_e4m3fn if fmt == "e4m3" else ml_dtypes.float8_e5m2).view(np.uint8)
    else:
        c = by_word.astype(ml_dtypes.float4_e2m1fn).view(np.uint8) & 0xF
        words = (c[..., 0::2] | (c[..., 1::2] << 4)).reshape(k // 512, 128, 2 * n)
    return np.ascontiguousarray(words), np.ascontiguousarray(byte.astype(np.uint8).reshape(k // 512, 16, n))


def unpack_weight(words, scales, fmt):
    g, _, n = scales.shape
    words = np.ascontiguousarray(words).reshape(g, 128, n, -1)
    if fmt in ("e4m3", "e5m2"):
        vals = words.view(ml_dtypes.float8_e4m3fn if fmt == "e4m3" else ml_dtypes.float8_e5m2).astype(np.float64)
    else:
        nib = np.empty((g, 128, n, 4), np.uint8)
        nib[..., 0::2] = words & 0xF
        nib[..., 1::2] = words >> 4
        vals = E2M1[nib]
    vals = vals * np.repeat(np.exp2(scales.astype(np.float64) - 127.0), 8, axis=1)[..., None]
    return vals.transpose(0, 1, 3, 2).reshape(g * 512, n)


K, T, J, R, F, Z, N, E = 512, 1024, 256, 512, 512, 1024, 256, 512


def setup_inputs():
    n = np.random.standard_normal
    idx = np.random.permutation(T)[:J]
    idx2 = np.random.permutation(Z)[:J]
    idx3 = np.stack([np.random.permutation(E)[:J] for _ in range(8)])
    idx4 = np.stack([np.random.permutation(E)[:J] for _ in range(8)])
    fk = mx_kscale(K)
    ff = mx_kscale(F)
    fr = mx_kscale(R)
    xtp = pack_weight(n((K, T)) / fk[:, None], "e4m3")
    xop = pack_weight(n((F, Z)) / ff[:, None], "e2m1")
    wp = pack_weight(n((K, R)) * 1 / np.sqrt(K) * fk[:, None] * fr, "e2m1")
    w0p = pack_weight(n((F, R)) * 1 / np.sqrt(F) * ff[:, None] * fr, "e5m2")
    w2p = pack_weight(n((F, R)) * 1 / np.sqrt(F) * ff[:, None] * fr, "e5m2")
    wbp = pack_weight(n((R, N)) * 1 / np.sqrt(R) / fr[:, None], "e5m2")
    wcp = pack_weight(n((R, N)) * 1 / np.sqrt(R) / fr[:, None], "e2m1")
    return {
        "xt_words": xtp[0],
        "xt_scales": xtp[1],
        "xo_words": xop[0],
        "xo_scales": xop[1],
        "w_words": wp[0],
        "w_scales": wp[1],
        "w0_words": w0p[0],
        "w0_scales": w0p[1],
        "w2_words": w2p[0],
        "w2_scales": w2p[1],
        "wb_words": wbp[0],
        "wb_scales": wbp[1],
        "wc_words": wcp[0],
        "wc_scales": wcp[1],
        "offs": striped(idx),
        "offs2": striped(idx2),
        "offs3": striped8(idx3),
        "offs4": striped8(idx4),
    }


def reference(xt_words, xt_scales, xo_words, xo_scales, w_words, w_scales, w0_words, w0_scales, w2_words, w2_scales, wb_words, wb_scales, wc_words, wc_scales, offs, offs2, offs3, offs4):
    idx = unstriped(offs)
    idx2 = unstriped(offs2)
    idx3 = unstriped8(offs3)
    idx4 = unstriped8(offs4)
    xtu = unpack_weight(xt_words, xt_scales, "e4m3")
    xou = unpack_weight(xo_words, xo_scales, "e2m1")
    wu = unpack_weight(w_words, w_scales, "e2m1")
    w0u = unpack_weight(w0_words, w0_scales, "e5m2")
    w2u = unpack_weight(w2_words, w2_scales, "e5m2")
    wbu = unpack_weight(wb_words, wb_scales, "e5m2")
    wcu = unpack_weight(wc_words, wc_scales, "e2m1")
    xtidxg = xtu[:, idx]
    xoidx2g = xou[:, idx2]
    a = wu.T @ xtidxg + w0u.T @ xoidx2g
    b = w2u.T @ xoidx2g
    hid = np.maximum(a, b)
    hidq = mxq(hid, 0, "e4m3")
    p = wbu.T @ hidq
    q = wcu.T @ hidq
    pw = np.zeros((N, E))
    pw[np.arange(N)[:, None], idx3[np.arange(N) % 128 // 16]] = p
    pv = np.zeros((N, E))
    pv[np.arange(N)[:, None], idx4[np.arange(N) % 128 // 16]] = q
    y = np.maximum(pw, pv)
    return y

@@ -1,0 +1,187 @@
+from contextlib import ExitStack
+
+import concourse.mybir as mybir
+from concourse.masks import make_identity
+
+K, T, J, R, F, Z, N, E = 512, 1024, 256, 512, 512, 1024, 256, 512
+FLOPS = 2 * J * (K * R + 2 * F * R + 2 * R * N)
+
+F32 = mybir.dt.float32
+BF16 = mybir.dt.bfloat16
+I32 = mybir.dt.int32
+U32 = mybir.dt.uint32
+U16 = mybir.dt.uint16
+U8 = mybir.dt.uint8
+E4M3 = mybir.dt.float8_e4m3fn_x4
+E5M2 = mybir.dt.float8_e5m2_x4
+E2M1 = mybir.dt.float4_e2m1fn_x4
+COPY = mybir.ActivationFunctionType.Copy
+MAX = mybir.AluOpType.max
+
+P = 128
+QUADS = 4
+ROWS = 4
+HALF = 128
+HALVES = J // HALF
+LIST_COLS = HALF // 16
+N_TILES = N // P
+
+
+def tile_list_outcomeownpages_noted_kernel(
+    tc, xt_words, xt_scales, xo_words, xo_scales, w_words, w_scales, w0_words, w0_scales,
+    w2_words, w2_scales, wb_words, wb_scales, wc_words, wc_scales, offs, offs2, offs3, offs4, out
+):
+    nc = tc.nc
+    with ExitStack() as ctx:
+        keep = ctx.enter_context(tc.tile_pool(name="keep", bufs=1))
+        psum = ctx.enter_context(tc.psum_pool(name="psum", bufs=1))
+
+        def load_list(name, src):
+            tile = keep.tile([P, J // 16], U16, name=name)
+            nc.sync.dma_start(tile[:], src)
+            return tile
+
+        def load_words(name, src, dtype, cols):
+            tile = keep.tile([P, cols], dtype, name=name, align_bytes=64)
+            nc.sync.dma_start(out=tile[:].bitcast(I32), in_=src.bitcast(I32))
+            return tile
+
+        def load_scales(name, src, cols):
+            staged = keep.tile([ROWS, QUADS, cols // 4], I32, name=name + "_staged")
+            nc.sync.dma_start(out=staged[:], in_=src[0].rearrange("(q r) n -> r q n", r=ROWS).bitcast(I32))
+            return staged
+
+        def clear_plane(name, cols):
+            plane = keep.tile([P, cols], U8, name=name + "_plane", align_bytes=64)
+            nc.vector.memset(plane[:].bitcast(I32), 0)
+            return plane
+
+        def spread(plane, staged):
+            for q in range(QUADS):
+                nc.vector.tensor_copy(out=plane[32 * q : 32 * q + ROWS, :].bitcast(I32), in_=staged[:, q, :])
+
+        def gather(name, window, dtype, offsets, h):
+            picked = keep.tile([P, HALF], dtype, name="%s_%d" % (name, h), align_bytes=64)
+            nc.vector.tensor_copy(
+                out=picked[:], in_=window.indirect(offsets[:, h * LIST_COLS : (h + 1) * LIST_COLS])
+            )
+            return picked
+
+        def fp8_rows(src):
+            return src[0].rearrange("p n t -> p (n t)")
+
+        xo_staged = load_scales("xo", xo_scales, Z)
+        w2_staged = load_scales("w2", w2_scales, R)
+        w0_staged = load_scales("w0", w0_scales, R)
+        list2 = load_list("list2", offs2)
+        xo_codes = load_words("xo_codes", xo_words[0], U16, Z)
+        w2_codes = load_words("w2_codes", fp8_rows(w2_words), I32, R)
+        xt_staged = load_scales("xt", xt_scales, T)
+        w_staged = load_scales("w", w_scales, R)
+        list1 = load_list("list1", offs)
+        w0_codes = load_words("w0_codes", fp8_rows(w0_words), I32, R)
+        xt_codes = load_words("xt_codes", fp8_rows(xt_words), I32, T)
+        w_codes = load_words("w_codes", w_words[0], U8, 2 * R)
+        wb_staged = load_scales("wb", wb_scales, N)
+        wc_staged = load_scales("wc", wc_scales, N)
+        wb_codes = load_words("wb_codes", fp8_rows(wb_words), I32, N)
+        wc_codes = load_words("wc_codes", wc_words[0], U8, 2 * N)
+        list3 = load_list("list3", offs3)
+        list4 = load_list("list4", offs4)
+
+        xo_plane = clear_plane("xo", Z)
+        w2_plane = clear_plane("w2", R)
+        w0_plane = clear_plane("w0", R)
+        xt_plane = clear_plane("xt", T)
+        w_plane = clear_plane("w", R)
+        wb_plane = clear_plane("wb", N)
+        wc_plane = clear_plane("wc", N)
+        pages = {}
+        for i in range(N_TILES):
+            for s in range(2):
+                pages[i, s] = keep.tile([P, E], F32, name="page_%d_%d" % (i, s))
+                nc.vector.memset(pages[i, s][:], 0.0)
+        identity = keep.tile([P, P], F32, name="identity")
+        make_identity(nc, identity[:])
+
+        def notes_part(h):
+            xo_s = gather("xo_s", xo_plane[:], U8, list2, h)
+            xo_c = gather("xo_c", xo_codes[:], U16, list2, h)
+            b_bank = psum.tile([P, R], F32, name="b_bank_%d" % h)
+            nc.tensor.matmul_mx(
+                out=b_bank[:], lhsT=xo_c[:].bitcast(E2M1), lhsT_scale=xo_s[:],
+                rhs=w2_codes[:].bitcast(E5M2), rhs_scale=w2_plane[:], start=True, stop=True,
+            )
+            a_bank = psum.tile([P, R], F32, name="a_bank_%d" % h)
+            nc.tensor.matmul_mx(
+                out=a_bank[:], lhsT=xo_c[:].bitcast(E2M1), lhsT_scale=xo_s[:],
+                rhs=w0_codes[:].bitcast(E5M2), rhs_scale=w0_plane[:], start=True, stop=False,
+            )
+            b_sb = keep.tile([P, 2, P, 2], F32, name="b_sb_%d" % h)
+            nc.scalar.activation(
+                out=b_sb[:], in_=b_bank[:].rearrange("j (p u e) -> j u p e", u=2, e=2), func=COPY
+            )
+            return a_bank, b_sb
+
+        def tokens_part(h, a_bank):
+            xt_s = gather("xt_s", xt_plane[:], U8, list1, h)
+            xt_c = gather("xt_c", xt_codes[:].bitcast(U32), U32, list1, h)
+            nc.tensor.matmul_mx(
+                out=a_bank[:], lhsT=xt_c[:].bitcast(E4M3), lhsT_scale=xt_s[:],
+                rhs=w_codes[:].bitcast(E2M1), rhs_scale=w_plane[:], start=False, stop=True,
+            )
+
+        def second_stage(h, a_bank, b_sb):
+            hid_t = keep.tile([P, 2, P, 2], BF16, name="hid_t_%d" % h, align_bytes=64)
+            nc.vector.tensor_tensor(
+                out=hid_t[:], in0=a_bank[:].rearrange("j (p u e) -> j u p e", u=2, e=2), in1=b_sb[:], op=MAX
+            )
+            pairs = hid_t[:].rearrange("j u p e -> j (u p e)").bitcast(F32)
+            turned = psum.tile([P, 2, HALF], F32, name="turned", tag="turned")
+            for u in range(2):
+                nc.tensor.transpose(turned[:, u, :], pairs[:, u * P : (u + 1) * P], identity[:])
+            hid = keep.tile([P, HALF * 4], BF16, name="hid_%d" % h, align_bytes=64)
+            nc.vector.tensor_copy(
+                out=hid[:].bitcast(F32).rearrange("p (j u) -> p j u", u=2),
+                in_=turned[:].rearrange("p u j -> p j u"),
+            )
+            hid_c = keep.tile([P, HALF], U32, name="hid_c_%d" % h, align_bytes=64)
+            hid_s = keep.tile([P, HALF], U8, name="hid_s_%d" % h, align_bytes=64)
+            nc.vector.quantize_mx(out=hid_c[:].bitcast(E4M3), scales=hid_s[:], in_=hid[:])
+            for i in range(N_TILES):
+                cols = slice(i * P, (i + 1) * P)
+                sides = (
+                    (wb_codes[:, cols].bitcast(E5M2), wb_plane, list3),
+                    (wc_codes[:, 2 * i * P : 2 * (i + 1) * P].bitcast(E2M1), wc_plane, list4),
+                )
+                for s, (codes, plane, offsets) in enumerate(sides):
+                    bank_tag = "outcome_%d" % min(2 * i + s, 2)
+                    bank = psum.tile([P, HALF], F32, name=bank_tag, tag=bank_tag)
+                    nc.tensor.matmul_mx(
+                        out=bank[:], lhsT=codes, lhsT_scale=plane[:, cols],
+                        rhs=hid_c[:].bitcast(E4M3), rhs_scale=hid_s[:], start=True, stop=True,
+                    )
+                    values = keep.tile([P, HALF], F32, name="values_%d_%d_%d" % (h, i, s))
+                    nc.vector.tensor_copy(out=values[:], in_=bank[:])
+                    nc.scalar.activation(
+                        out=pages[i, s][:].indirect(offsets[:, h * LIST_COLS : (h + 1) * LIST_COLS]),
+                        in_=values[:], func=COPY,
+                    )
+                if h == HALVES - 1:
+                    result = keep.tile([P, E], F32, name="result_%d" % i)
+                    nc.vector.tensor_tensor(out=result[:], in0=pages[i, 0][:], in1=pages[i, 1][:], op=MAX)
+                    nc.sync.dma_start(out=out[cols, :], in_=result[:])
+
+        spread(xo_plane, xo_staged)
+        spread(w2_plane, w2_staged)
+        spread(w0_plane, w0_staged)
+        first = [notes_part(0)]
+        spread(xt_plane, xt_staged)
+        spread(w_plane, w_staged)
+        tokens_part(0, first[0][0])
+        first.append(notes_part(1))
+        spread(wb_plane, wb_staged)
+        spread(wc_plane, wc_staged)
+        second_stage(0, *first[0])
+        tokens_part(1, first[1][0])
+        second_stage(1, *first[1])

@@ -1,7 +1,6 @@
 from contextlib import ExitStack
 
 import concourse.mybir as mybir
-from concourse.masks import make_identity
 
 K, T, J, R, F, Z, N, E = 512, 1024, 256, 512, 512, 1024, 256, 512
 FLOPS = 2 * J * (K * R + 2 * F * R + 2 * R * N)
@@ -21,10 +20,12 @@ MAX = mybir.AluOpType.max
 P = 128
 QUADS = 4
 ROWS = 4
+PACK = 4
 HALF = 128
 HALVES = J // HALF
 LIST_COLS = HALF // 16
 N_TILES = N // P
+LINE = 16
 
 
 def tile_list_outcomeownpages_noted_kernel(
@@ -46,22 +47,23 @@ def tile_list_outcomeownpages_noted_kernel(
             nc.sync.dma_start(out=tile[:].bitcast(I32), in_=src.bitcast(I32))
             return tile
 
-        def load_scales(name, src, cols):
-            staged = keep.tile([ROWS, QUADS, cols // 4], I32, name=name + "_staged")
-            nc.sync.dma_start(out=staged[:], in_=src[0].rearrange("(q r) n -> r q n", r=ROWS).bitcast(I32))
-            return staged
-
-        def clear_plane(name, cols):
-            plane = keep.tile([P, cols], U8, name=name + "_plane", align_bytes=64)
-            nc.vector.memset(plane[:].bitcast(I32), 0)
-            return plane
+        def load_scale_rows(staged, src):
+            nc.sync.dma_start(out=staged, in_=src[0].rearrange("(q r) n -> r q n", r=ROWS).bitcast(I32))
 
         def spread(plane, staged):
             for q in range(QUADS):
                 nc.vector.tensor_copy(out=plane[32 * q : 32 * q + ROWS, :].bitcast(I32), in_=staged[:, q, :])
 
-        def gather(name, window, dtype, offsets, h):
-            picked = keep.tile([P, HALF], dtype, name="%s_%d" % (name, h), align_bytes=64)
+        def deal(copy, name, src, dtype, run):
+            dealt = keep.tile([P, R], dtype, name=name, align_bytes=64)
+            copy(
+                out=dealt[:].rearrange("p (t b i) -> p b t i", t=PACK, i=run),
+                in_=src.rearrange("p (b i t) -> p b t i", t=PACK, i=run),
+            )
+            return dealt
+
+        def gather(name, window, dtype, offsets, h, tag=""):
+            picked = keep.tile([P, HALF], dtype, name="%s_%d" % (name, h), tag=tag, align_bytes=64)
             nc.vector.tensor_copy(
                 out=picked[:], in_=window.indirect(offsets[:, h * LIST_COLS : (h + 1) * LIST_COLS])
             )
@@ -70,118 +72,129 @@ def tile_list_outcomeownpages_noted_kernel(
         def fp8_rows(src):
             return src[0].rearrange("p n t -> p (n t)")
 
-        xo_staged = load_scales("xo", xo_scales, Z)
-        w2_staged = load_scales("w2", w2_scales, R)
-        w0_staged = load_scales("w0", w0_scales, R)
+        xt_plane = keep.tile([P, T], U8, name="xt_plane", align_bytes=64)
+        nc.vector.memset(xt_plane[:].bitcast(I32), 0)
+        xo_staged = keep.tile([ROWS, QUADS, Z // 4], I32, name="xo_staged")
+        xo_plane = keep.tile([P, Z], U8, name="xo_plane", align_bytes=64)
+        nc.vector.memset(xo_plane[:].bitcast(I32), 0)
+        first_staged = keep.tile([ROWS, QUADS, 3 * R // 4], I32, name="first_staged")
+        first_plane = keep.tile([P, 3 * R], U8, name="first_plane", align_bytes=64)
+        nc.vector.memset(first_plane[:].bitcast(I32), 0)
+        second_staged = keep.tile([ROWS, QUADS, 2 * N // 4], I32, name="second_staged")
+        second_plane = keep.tile([P, 2 * N], U8, name="second_plane", align_bytes=64)
+        nc.vector.memset(second_plane[:].bitcast(I32), 0)
+        pages = {}
+
+        for n, src in enumerate((w2_scales, w0_scales, w_scales)):
+            load_scale_rows(first_staged[:, :, n * R // 4 : (n + 1) * R // 4], src)
+        load_scale_rows(xo_staged[:], xo_scales)
         list2 = load_list("list2", offs2)
+        w2_codes = load_words("w2_codes", fp8_rows(w2_words), U32, R)
         xo_codes = load_words("xo_codes", xo_words[0], U16, Z)
-        w2_codes = load_words("w2_codes", fp8_rows(w2_words), I32, R)
-        xt_staged = load_scales("xt", xt_scales, T)
-        w_staged = load_scales("w", w_scales, R)
+        w0_codes = load_words("w0_codes", fp8_rows(w0_words), U32, R)
+        w_codes = load_words("w_codes", w_words[0], U16, R)
         list1 = load_list("list1", offs)
-        w0_codes = load_words("w0_codes", fp8_rows(w0_words), I32, R)
-        xt_codes = load_words("xt_codes", fp8_rows(xt_words), I32, T)
-        w_codes = load_words("w_codes", w_words[0], U8, 2 * R)
-        wb_staged = load_scales("wb", wb_scales, N)
-        wc_staged = load_scales("wc", wc_scales, N)
-        wb_codes = load_words("wb_codes", fp8_rows(wb_words), I32, N)
-        wc_codes = load_words("wc_codes", wc_words[0], U8, 2 * N)
+        xt_codes = load_words("xt_codes", fp8_rows(xt_words), U32, T)
+        for q in range(QUADS):
+            nc.sync.dma_start(
+                out=xt_plane[32 * q : 32 * q + ROWS, :].bitcast(I32),
+                in_=xt_scales[0, ROWS * q : ROWS * (q + 1), :].bitcast(I32),
+            )
+        for n, src in enumerate((wb_scales, wc_scales)):
+            load_scale_rows(second_staged[:, :, n * N // 4 : (n + 1) * N // 4], src)
+        wb_codes = load_words("wb_codes", fp8_rows(wb_words), U32, N)
+        wc_codes = load_words("wc_codes", wc_words[0], U16, N)
         list3 = load_list("list3", offs3)
         list4 = load_list("list4", offs4)
 
-        xo_plane = clear_plane("xo", Z)
-        w2_plane = clear_plane("w2", R)
-        w0_plane = clear_plane("w0", R)
-        xt_plane = clear_plane("xt", T)
-        w_plane = clear_plane("w", R)
-        wb_plane = clear_plane("wb", N)
-        wc_plane = clear_plane("wc", N)
-        pages = {}
-        for i in range(N_TILES):
-            for s in range(2):
-                pages[i, s] = keep.tile([P, E], F32, name="page_%d_%d" % (i, s))
-                nc.vector.memset(pages[i, s][:], 0.0)
-        identity = keep.tile([P, P], F32, name="identity")
-        make_identity(nc, identity[:])
+        def one_pass(bank, t, weight, moving, start=False, stop=False):
+            codes, scales, fmt = weight
+            cols = slice(t * P, (t + 1) * P)
+            nc.tensor.matmul_mx(
+                out=bank[:, t, :], lhsT=codes[:, cols].bitcast(fmt), lhsT_scale=scales[:, cols],
+                rhs=moving[0], rhs_scale=moving[1], start=start, stop=stop,
+            )
 
         def notes_part(h):
-            xo_s = gather("xo_s", xo_plane[:], U8, list2, h)
-            xo_c = gather("xo_c", xo_codes[:], U16, list2, h)
-            b_bank = psum.tile([P, R], F32, name="b_bank_%d" % h)
-            nc.tensor.matmul_mx(
-                out=b_bank[:], lhsT=xo_c[:].bitcast(E2M1), lhsT_scale=xo_s[:],
-                rhs=w2_codes[:].bitcast(E5M2), rhs_scale=w2_plane[:], start=True, stop=True,
-            )
-            a_bank = psum.tile([P, R], F32, name="a_bank_%d" % h)
-            nc.tensor.matmul_mx(
-                out=a_bank[:], lhsT=xo_c[:].bitcast(E2M1), lhsT_scale=xo_s[:],
-                rhs=w0_codes[:].bitcast(E5M2), rhs_scale=w0_plane[:], start=True, stop=False,
-            )
-            b_sb = keep.tile([P, 2, P, 2], F32, name="b_sb_%d" % h)
-            nc.scalar.activation(
-                out=b_sb[:], in_=b_bank[:].rearrange("j (p u e) -> j u p e", u=2, e=2), func=COPY
-            )
-            return a_bank, b_sb
+            xo_s = gather("xo_s", xo_plane[:], U8, list2, h, tag="xo_s")
+            xo_c = gather("xo_c", xo_codes[:], U16, list2, h, tag="xo_c")
+            b_bank = psum.tile([P, PACK, HALF], F32, name="b_bank_%d" % h)
+            for t in range(PACK):
+                one_pass(b_bank, t, (w2_dealt, w2_plane, E5M2), (xo_c[:].bitcast(E2M1), xo_s[:]), True, True)
+            b_sb = keep.tile([P, HALF, PACK], F32, name="b_sb_%d" % h, tag="b_sb_%d" % h, align_bytes=64)
+            nc.scalar.activation(out=b_sb[:], in_=b_bank[:].rearrange("p t j -> p j t"), func=COPY)
+            return xo_c, xo_s, b_sb
 
-        def tokens_part(h, a_bank):
-            xt_s = gather("xt_s", xt_plane[:], U8, list1, h)
-            xt_c = gather("xt_c", xt_codes[:].bitcast(U32), U32, list1, h)
-            nc.tensor.matmul_mx(
-                out=a_bank[:], lhsT=xt_c[:].bitcast(E4M3), lhsT_scale=xt_s[:],
-                rhs=w_codes[:].bitcast(E2M1), rhs_scale=w_plane[:], start=False, stop=True,
-            )
+        def tokens_part(h, xo_c, xo_s):
+            a_bank = psum.tile([P, PACK, HALF], F32, name="a_bank_%d" % h)
+            notes = (xo_c[:].bitcast(E2M1), xo_s[:])
+            last = PACK - 1
+            for t in range(last):
+                one_pass(a_bank, t, (w0_dealt, w0_plane, E5M2), notes, start=t == 0)
+            xt_c = gather("xt_c", xt_codes[:], U32, list1, h, tag="hid_0" if h else "")
+            xt_s = gather("xt_s", xt_plane[:], U8, list1, h, tag="b_sb_0" if h else "")
+            tokens = (xt_c[:].bitcast(E4M3), xt_s[:])
+            one_pass(a_bank, last, (w_dealt, w_plane, E2M1), tokens)
+            one_pass(a_bank, last, (w0_dealt, w0_plane, E5M2), notes)
+            for t in range(last):
+                one_pass(a_bank, t, (w_dealt, w_plane, E2M1), tokens, stop=t == last - 1)
+            return a_bank
 
         def second_stage(h, a_bank, b_sb):
-            hid_t = keep.tile([P, 2, P, 2], BF16, name="hid_t_%d" % h, align_bytes=64)
+            hid = keep.tile([P, HALF * PACK], BF16, name="hid_%d" % h, tag="hid_%d" % h, align_bytes=64)
             nc.vector.tensor_tensor(
-                out=hid_t[:], in0=a_bank[:].rearrange("j (p u e) -> j u p e", u=2, e=2), in1=b_sb[:], op=MAX
+                out=hid[:].rearrange("p (j t) -> p j t", t=PACK),
+                in0=a_bank[:].rearrange("p t j -> p j t"), in1=b_sb[:], op=MAX,
             )
-            pairs = hid_t[:].rearrange("j u p e -> j (u p e)").bitcast(F32)
-            turned = psum.tile([P, 2, HALF], F32, name="turned", tag="turned")
-            for u in range(2):
-                nc.tensor.transpose(turned[:, u, :], pairs[:, u * P : (u + 1) * P], identity[:])
-            hid = keep.tile([P, HALF * 4], BF16, name="hid_%d" % h, align_bytes=64)
-            nc.vector.tensor_copy(
-                out=hid[:].bitcast(F32).rearrange("p (j u) -> p j u", u=2),
-                in_=turned[:].rearrange("p u j -> p j u"),
-            )
+            if h == 0:
+                spread(second_plane, second_staged)
             hid_c = keep.tile([P, HALF], U32, name="hid_c_%d" % h, align_bytes=64)
             hid_s = keep.tile([P, HALF], U8, name="hid_s_%d" % h, align_bytes=64)
             nc.vector.quantize_mx(out=hid_c[:].bitcast(E4M3), scales=hid_s[:], in_=hid[:])
             for i in range(N_TILES):
                 cols = slice(i * P, (i + 1) * P)
-                sides = (
-                    (wb_codes[:, cols].bitcast(E5M2), wb_plane, list3),
-                    (wc_codes[:, 2 * i * P : 2 * (i + 1) * P].bitcast(E2M1), wc_plane, list4),
-                )
-                for s, (codes, plane, offsets) in enumerate(sides):
-                    bank_tag = "outcome_%d" % min(2 * i + s, 2)
+                sides = ((wb_codes, E5M2, list3), (wc_codes, E2M1, list4))
+                for s, (codes, fmt, offsets) in enumerate(sides):
+                    bank_tag = "outcome_%d_%d" % (i, s)
                     bank = psum.tile([P, HALF], F32, name=bank_tag, tag=bank_tag)
                     nc.tensor.matmul_mx(
-                        out=bank[:], lhsT=codes, lhsT_scale=plane[:, cols],
+                        out=bank[:], lhsT=codes[:, cols].bitcast(fmt),
+                        lhsT_scale=second_plane[:, s * N + i * P : s * N + (i + 1) * P],
                         rhs=hid_c[:].bitcast(E4M3), rhs_scale=hid_s[:], start=True, stop=True,
                     )
                     values = keep.tile([P, HALF], F32, name="values_%d_%d_%d" % (h, i, s))
-                    nc.vector.tensor_copy(out=values[:], in_=bank[:])
+                    if h + i + s == 0:
+                        nc.scalar.activation(out=values[:], in_=bank[:], func=COPY)
+                    else:
+                        nc.vector.tensor_copy(out=values[:], in_=bank[:])
+                    if h == 0:
+                        pages[i, s] = keep.tile([P, E], F32, name="page_%d_%d" % (i, s))
+                        (nc.vector if i == 0 else nc.gpsimd).memset(pages[i, s][:].bitcast(I32), 0)
                     nc.scalar.activation(
                         out=pages[i, s][:].indirect(offsets[:, h * LIST_COLS : (h + 1) * LIST_COLS]),
                         in_=values[:], func=COPY,
                     )
                 if h == HALVES - 1:
-                    result = keep.tile([P, E], F32, name="result_%d" % i)
-                    nc.vector.tensor_tensor(out=result[:], in0=pages[i, 0][:], in1=pages[i, 1][:], op=MAX)
-                    nc.sync.dma_start(out=out[cols, :], in_=result[:])
+                    pieces = 1 if i < N_TILES - 1 else 2
+                    for c in range(pieces):
+                        part = slice(c * E // pieces, (c + 1) * E // pieces)
+                        result = keep.tile([P, E // pieces], F32, name="result_%d_%d" % (i, c))
+                        nc.vector.tensor_tensor(
+                            out=result[:], in0=pages[i, 0][:, part], in1=pages[i, 1][:, part], op=MAX
+                        )
+                        (nc.scalar if c else nc.sync).dma_start(out=out[cols, part], in_=result[:])
 
+        spread(first_plane, first_staged)
         spread(xo_plane, xo_staged)
-        spread(w2_plane, w2_staged)
-        spread(w0_plane, w0_staged)
-        first = [notes_part(0)]
-        spread(xt_plane, xt_staged)
-        spread(w_plane, w_staged)
-        tokens_part(0, first[0][0])
-        first.append(notes_part(1))
-        spread(wb_plane, wb_staged)
-        spread(wc_plane, wc_staged)
-        second_stage(0, *first[0])
-        tokens_part(1, first[1][0])
-        second_stage(1, *first[1])
+        w2_plane = deal(nc.vector.tensor_copy, "w2_plane", first_plane[:, 0:R], U8, LINE)
+        w2_dealt = deal(nc.scalar.copy, "w2_dealt", w2_codes[:], U32, LINE // 4)
+        w0_dealt = deal(nc.scalar.copy, "w0_dealt", w0_codes[:], U32, LINE // 4)
+        w_dealt = deal(nc.scalar.copy, "w_dealt", w_codes[:], U16, LINE // 2)
+        xo_c, xo_s, b_sb = notes_part(0)
+        w0_plane = deal(nc.vector.tensor_copy, "w0_plane", first_plane[:, R : 2 * R], U8, LINE)
+        w_plane = deal(nc.vector.tensor_copy, "w_plane", first_plane[:, 2 * R : 3 * R], U8, LINE)
+        a_bank = tokens_part(0, xo_c, xo_s)
+        xo_c, xo_s, b_next = notes_part(1)
+        second_stage(0, a_bank, b_sb)
+        a_bank = tokens_part(1, xo_c, xo_s)
+        second_stage(1, a_bank, b_next)

@@ -85,9 +85,9 @@ def tile_list_outcomeownpages_noted_kernel(
         nc.vector.memset(second_plane[:].bitcast(I32), 0)
         pages = {}
 
+        load_scale_rows(xo_staged[:], xo_scales)
         for n, src in enumerate((w2_scales, w0_scales, w_scales)):
             load_scale_rows(first_staged[:, :, n * R // 4 : (n + 1) * R // 4], src)
-        load_scale_rows(xo_staged[:], xo_scales)
         list2 = load_list("list2", offs2)
         w2_codes = load_words("w2_codes", fp8_rows(w2_words), U32, R)
         xo_codes = load_words("xo_codes", xo_words[0], U16, Z)
@@ -95,10 +95,10 @@ def tile_list_outcomeownpages_noted_kernel(
         w_codes = load_words("w_codes", w_words[0], U16, R)
         list1 = load_list("list1", offs)
         xt_codes = load_words("xt_codes", fp8_rows(xt_words), U32, T)
-        for q in range(QUADS):
+        for r in range(ROWS):
             nc.sync.dma_start(
-                out=xt_plane[32 * q : 32 * q + ROWS, :].bitcast(I32),
-                in_=xt_scales[0, ROWS * q : ROWS * (q + 1), :].bitcast(I32),
+                out=xt_plane[r:P:32, :].bitcast(I32),
+                in_=xt_scales[0, r : ROWS * QUADS : ROWS, :].bitcast(I32),
             )
         for n, src in enumerate((wb_scales, wc_scales)):
             load_scale_rows(second_staged[:, :, n * N // 4 : (n + 1) * N // 4], src)
@@ -169,7 +169,7 @@ def tile_list_outcomeownpages_noted_kernel(
                         nc.vector.tensor_copy(out=values[:], in_=bank[:])
                     if h == 0:
                         pages[i, s] = keep.tile([P, E], F32, name="page_%d_%d" % (i, s))
-                        (nc.vector if i == 0 else nc.gpsimd).memset(pages[i, s][:].bitcast(I32), 0)
+                        (nc.vector if i + s == 0 else nc.gpsimd).memset(pages[i, s][:].bitcast(I32), 0)
                     nc.scalar.activation(
                         out=pages[i, s][:].indirect(offsets[:, h * LIST_COLS : (h + 1) * LIST_COLS]),
                         in_=values[:], func=COPY,
@@ -184,15 +184,15 @@ def tile_list_outcomeownpages_noted_kernel(
                         )
                         (nc.scalar if c else nc.sync).dma_start(out=out[cols, part], in_=result[:])
 
-        spread(first_plane, first_staged)
         spread(xo_plane, xo_staged)
+        spread(first_plane, first_staged)
         w2_plane = deal(nc.vector.tensor_copy, "w2_plane", first_plane[:, 0:R], U8, LINE)
         w2_dealt = deal(nc.scalar.copy, "w2_dealt", w2_codes[:], U32, LINE // 4)
         w0_dealt = deal(nc.scalar.copy, "w0_dealt", w0_codes[:], U32, LINE // 4)
         w_dealt = deal(nc.scalar.copy, "w_dealt", w_codes[:], U16, LINE // 2)
         xo_c, xo_s, b_sb = notes_part(0)
-        w0_plane = deal(nc.vector.tensor_copy, "w0_plane", first_plane[:, R : 2 * R], U8, LINE)
-        w_plane = deal(nc.vector.tensor_copy, "w_plane", first_plane[:, 2 * R : 3 * R], U8, LINE)
+        w0_plane = deal(nc.gpsimd.tensor_copy, "w0_plane", first_plane[:, R : 2 * R], U8, P)
+        w_plane = deal(nc.gpsimd.tensor_copy, "w_plane", first_plane[:, 2 * R : 3 * R], U8, P)
         a_bank = tokens_part(0, xo_c, xo_s)
         xo_c, xo_s, b_next = notes_part(1)
         second_stage(0, a_bank, b_sb)

from contextlib import ExitStack

import concourse.mybir as mybir

K, T, J, R, F, Z, N, E = 512, 1024, 256, 512, 512, 1024, 256, 512
FLOPS = 2 * J * (K * R + 2 * F * R + 2 * R * N)

F32 = mybir.dt.float32
BF16 = mybir.dt.bfloat16
I32 = mybir.dt.int32
U32 = mybir.dt.uint32
U16 = mybir.dt.uint16
U8 = mybir.dt.uint8
E4M3 = mybir.dt.float8_e4m3fn_x4
E5M2 = mybir.dt.float8_e5m2_x4
E2M1 = mybir.dt.float4_e2m1fn_x4
COPY = mybir.ActivationFunctionType.Copy
MAX = mybir.AluOpType.max

P = 128
QUADS = 4
ROWS = 4
PACK = 4
HALF = 128
HALVES = J // HALF
LIST_COLS = HALF // 16
N_TILES = N // P
LINE = 16


def tile_list_outcomeownpages_noted_kernel(
    tc, xt_words, xt_scales, xo_words, xo_scales, w_words, w_scales, w0_words, w0_scales,
    w2_words, w2_scales, wb_words, wb_scales, wc_words, wc_scales, offs, offs2, offs3, offs4, out
):
    nc = tc.nc
    with ExitStack() as ctx:
        keep = ctx.enter_context(tc.tile_pool(name="keep", bufs=1))
        psum = ctx.enter_context(tc.psum_pool(name="psum", bufs=1))

        def load_list(name, src):
            tile = keep.tile([P, J // 16], U16, name=name)
            nc.sync.dma_start(tile[:], src)
            return tile

        def load_words(name, src, dtype, cols):
            tile = keep.tile([P, cols], dtype, name=name, align_bytes=64)
            nc.sync.dma_start(out=tile[:].bitcast(I32), in_=src.bitcast(I32))
            return tile

        def load_scale_rows(staged, src):
            nc.sync.dma_start(out=staged, in_=src[0].rearrange("(q r) n -> r q n", r=ROWS).bitcast(I32))

        def spread(plane, staged):
            for q in range(QUADS):
                nc.vector.tensor_copy(out=plane[32 * q : 32 * q + ROWS, :].bitcast(I32), in_=staged[:, q, :])

        def deal(copy, name, src, dtype, run):
            dealt = keep.tile([P, R], dtype, name=name, align_bytes=64)
            copy(
                out=dealt[:].rearrange("p (t b i) -> p b t i", t=PACK, i=run),
                in_=src.rearrange("p (b i t) -> p b t i", t=PACK, i=run),
            )
            return dealt

        def gather(name, window, dtype, offsets, h, tag=""):
            picked = keep.tile([P, HALF], dtype, name="%s_%d" % (name, h), tag=tag, align_bytes=64)
            nc.vector.tensor_copy(
                out=picked[:], in_=window.indirect(offsets[:, h * LIST_COLS : (h + 1) * LIST_COLS])
            )
            return picked

        def fp8_rows(src):
            return src[0].rearrange("p n t -> p (n t)")

        xt_plane = keep.tile([P, T], U8, name="xt_plane", align_bytes=64)
        nc.vector.memset(xt_plane[:].bitcast(I32), 0)
        xo_staged = keep.tile([ROWS, QUADS, Z // 4], I32, name="xo_staged")
        xo_plane = keep.tile([P, Z], U8, name="xo_plane", align_bytes=64)
        nc.vector.memset(xo_plane[:].bitcast(I32), 0)
        first_staged = keep.tile([ROWS, QUADS, 3 * R // 4], I32, name="first_staged")
        first_plane = keep.tile([P, 3 * R], U8, name="first_plane", align_bytes=64)
        nc.vector.memset(first_plane[:].bitcast(I32), 0)
        second_staged = keep.tile([ROWS, QUADS, 2 * N // 4], I32, name="second_staged")
        second_plane = keep.tile([P, 2 * N], U8, name="second_plane", align_bytes=64)
        nc.vector.memset(second_plane[:].bitcast(I32), 0)
        pages = {}

        load_scale_rows(xo_staged[:], xo_scales)
        for n, src in enumerate((w2_scales, w0_scales, w_scales)):
            load_scale_rows(first_staged[:, :, n * R // 4 : (n + 1) * R // 4], src)
        list2 = load_list("list2", offs2)
        w2_codes = load_words("w2_codes", fp8_rows(w2_words), U32, R)
        xo_codes = load_words("xo_codes", xo_words[0], U16, Z)
        w0_codes = load_words("w0_codes", fp8_rows(w0_words), U32, R)
        w_codes = load_words("w_codes", w_words[0], U16, R)
        list1 = load_list("list1", offs)
        xt_codes = load_words("xt_codes", fp8_rows(xt_words), U32, T)
        for r in range(ROWS):
            nc.sync.dma_start(
                out=xt_plane[r:P:32, :].bitcast(I32),
                in_=xt_scales[0, r : ROWS * QUADS : ROWS, :].bitcast(I32),
            )
        for n, src in enumerate((wb_scales, wc_scales)):
            load_scale_rows(second_staged[:, :, n * N // 4 : (n + 1) * N // 4], src)
        wb_codes = load_words("wb_codes", fp8_rows(wb_words), U32, N)
        wc_codes = load_words("wc_codes", wc_words[0], U16, N)
        list3 = load_list("list3", offs3)
        list4 = load_list("list4", offs4)

        def one_pass(bank, t, weight, moving, start=False, stop=False):
            codes, scales, fmt = weight
            cols = slice(t * P, (t + 1) * P)
            nc.tensor.matmul_mx(
                out=bank[:, t, :], lhsT=codes[:, cols].bitcast(fmt), lhsT_scale=scales[:, cols],
                rhs=moving[0], rhs_scale=moving[1], start=start, stop=stop,
            )

        def notes_part(h):
            xo_s = gather("xo_s", xo_plane[:], U8, list2, h, tag="xo_s")
            xo_c = gather("xo_c", xo_codes[:], U16, list2, h, tag="xo_c")
            b_bank = psum.tile([P, PACK, HALF], F32, name="b_bank_%d" % h)
            for t in range(PACK):
                one_pass(b_bank, t, (w2_dealt, w2_plane, E5M2), (xo_c[:].bitcast(E2M1), xo_s[:]), True, True)
            b_sb = keep.tile([P, HALF, PACK], F32, name="b_sb_%d" % h, tag="b_sb_%d" % h, align_bytes=64)
            nc.scalar.activation(out=b_sb[:], in_=b_bank[:].rearrange("p t j -> p j t"), func=COPY)
            return xo_c, xo_s, b_sb

        def tokens_part(h, xo_c, xo_s):
            a_bank = psum.tile([P, PACK, HALF], F32, name="a_bank_%d" % h)
            notes = (xo_c[:].bitcast(E2M1), xo_s[:])
            last = PACK - 1
            for t in range(last):
                one_pass(a_bank, t, (w0_dealt, w0_plane, E5M2), notes, start=t == 0)
            xt_c = gather("xt_c", xt_codes[:], U32, list1, h, tag="hid_0" if h else "")
            xt_s = gather("xt_s", xt_plane[:], U8, list1, h, tag="b_sb_0" if h else "")
            tokens = (xt_c[:].bitcast(E4M3), xt_s[:])
            one_pass(a_bank, last, (w_dealt, w_plane, E2M1), tokens)
            one_pass(a_bank, last, (w0_dealt, w0_plane, E5M2), notes)
            for t in range(last):
                one_pass(a_bank, t, (w_dealt, w_plane, E2M1), tokens, stop=t == last - 1)
            return a_bank

        def second_stage(h, a_bank, b_sb):
            hid = keep.tile([P, HALF * PACK], BF16, name="hid_%d" % h, tag="hid_%d" % h, align_bytes=64)
            nc.vector.tensor_tensor(
                out=hid[:].rearrange("p (j t) -> p j t", t=PACK),
                in0=a_bank[:].rearrange("p t j -> p j t"), in1=b_sb[:], op=MAX,
            )
            if h == 0:
                spread(second_plane, second_staged)
            hid_c = keep.tile([P, HALF], U32, name="hid_c_%d" % h, align_bytes=64)
            hid_s = keep.tile([P, HALF], U8, name="hid_s_%d" % h, align_bytes=64)
            nc.vector.quantize_mx(out=hid_c[:].bitcast(E4M3), scales=hid_s[:], in_=hid[:])
            for i in range(N_TILES):
                cols = slice(i * P, (i + 1) * P)
                sides = ((wb_codes, E5M2, list3), (wc_codes, E2M1, list4))
                for s, (codes, fmt, offsets) in enumerate(sides):
                    bank_tag = "outcome_%d_%d" % (i, s)
                    bank = psum.tile([P, HALF], F32, name=bank_tag, tag=bank_tag)
                    nc.tensor.matmul_mx(
                        out=bank[:], lhsT=codes[:, cols].bitcast(fmt),
                        lhsT_scale=second_plane[:, s * N + i * P : s * N + (i + 1) * P],
                        rhs=hid_c[:].bitcast(E4M3), rhs_scale=hid_s[:], start=True, stop=True,
                    )
                    values = keep.tile([P, HALF], F32, name="values_%d_%d_%d" % (h, i, s))
                    if h + i + s == 0:
                        nc.scalar.activation(out=values[:], in_=bank[:], func=COPY)
                    else:
                        nc.vector.tensor_copy(out=values[:], in_=bank[:])
                    if h == 0:
                        pages[i, s] = keep.tile([P, E], F32, name="page_%d_%d" % (i, s))
                        (nc.vector if i + s == 0 else nc.gpsimd).memset(pages[i, s][:].bitcast(I32), 0)
                    nc.scalar.activation(
                        out=pages[i, s][:].indirect(offsets[:, h * LIST_COLS : (h + 1) * LIST_COLS]),
                        in_=values[:], func=COPY,
                    )
                if h == HALVES - 1:
                    pieces = 1 if i < N_TILES - 1 else 2
                    for c in range(pieces):
                        part = slice(c * E // pieces, (c + 1) * E // pieces)
                        result = keep.tile([P, E // pieces], F32, name="result_%d_%d" % (i, c))
                        nc.vector.tensor_tensor(
                            out=result[:], in0=pages[i, 0][:, part], in1=pages[i, 1][:, part], op=MAX
                        )
                        (nc.scalar if c else nc.sync).dma_start(out=out[cols, part], in_=result[:])

        spread(xo_plane, xo_staged)
        spread(first_plane, first_staged)
        w2_plane = deal(nc.vector.tensor_copy, "w2_plane", first_plane[:, 0:R], U8, LINE)
        w2_dealt = deal(nc.scalar.copy, "w2_dealt", w2_codes[:], U32, LINE // 4)
        w0_dealt = deal(nc.scalar.copy, "w0_dealt", w0_codes[:], U32, LINE // 4)
        w_dealt = deal(nc.scalar.copy, "w_dealt", w_codes[:], U16, LINE // 2)
        xo_c, xo_s, b_sb = notes_part(0)
        w0_plane = deal(nc.gpsimd.tensor_copy, "w0_plane", first_plane[:, R : 2 * R], U8, P)
        w_plane = deal(nc.gpsimd.tensor_copy, "w_plane", first_plane[:, 2 * R : 3 * R], U8, P)
        a_bank = tokens_part(0, xo_c, xo_s)
        xo_c, xo_s, b_next = notes_part(1)
        second_stage(0, a_bank, b_sb)
        a_bank = tokens_part(1, xo_c, xo_s)
        second_stage(1, a_bank, b_next)
